import numpy as np
CORES = [2,34,66,98,130,162,194,226,258,290,322,354,386,418,450,482]
N = 16
F = 64
def setup_inputs(rng):
    m = (rng.standard_normal((N, 128, 128), dtype=np.float32) / 11)
    return {"m": m, "mt": m.transpose(0, 2, 1).copy(), "x": rng.standard_normal((N, 128, F), dtype=np.float32)}
def setup_inputs_big(rng):
    d = setup_inputs(rng)
    for k in ("x",): d[k] = (d[k].astype(np.float32) * 1048576.0).astype(d[k].dtype)
    return d
def setup_inputs_small(rng):
    d = setup_inputs(rng)
    for k in ("x",): d[k] = (d[k].astype(np.float32) * (1 / 1048576.0)).astype(d[k].dtype)
    return d
def setup_inputs_apart(rng):
    d = setup_inputs(rng)
    f = (10.0 ** rng.permutation(np.linspace(-1.5, 1.5, N))).astype(np.float32).reshape(N, 1, 1)
    for k in ("x",): d[k] = (d[k].astype(np.float32) * f).astype(d[k].dtype)
    return d
def reference(m, mt, x):
    M, X = m.astype(np.float64), x.astype(np.float64)
    y = np.zeros((N, 128, F)); p = X[0]
    for r in range(N):
        p = M[r].T @ p
        y[r] = p
    return {"y": y.astype(np.float32)}

@@ -1,0 +1,180 @@
+from concourse.bass import DstId, RemoteDMATransfer
+
+W = 128
+NPROD = 6
+
+SCRATCH = {
+    "gat": ("sbuf", [128, 4 * W], "float32"),
+    "own2": ("sbuf", [128, W], "float32"),
+    "xin": ("sbuf", [128, 64], "float32"),
+    "pl": ("sbuf", [128, 64], "float32"),
+    "gl": ("sbuf", [128, W], "float32"),
+}
+for _k in range(NPROD):
+    SCRATCH["ps%d" % _k] = ("psum", [128, 512], "float32")
+    SCRATCH["sb%d" % _k] = ("sbuf", [128, W], "float32")
+
+SEMAPHORES = (["ld_a", "ld_b", "ld_x", "a0", "a1", "a2", "a3", "a_p", "a_g", "s1", "s2", "s3", "stored"]
+              + ["t%d" % _k for _k in range(NPROD)] + ["v%d" % _k for _k in range(NPROD)])
+
+
+def rank_program(g, core, T, topo):
+    if T.rank_of(core) is None:
+        return
+    cores = list(T.cores)
+    hosts = []
+    for c in cores:
+        if topo.host(c) not in hosts:
+            hosts.append(topo.host(c))
+    groups = [[c for c in cores if topo.host(c) == h] for h in hosts]
+    gi = hosts.index(topo.host(core))
+    grp = groups[gi]
+    j = grp.index(core)
+    F = T.y.shape[1]
+    last = len(groups) - 1
+
+    queues = {"g": g, "tensor": g.tensor, "vector": g.vector, "sync": g.sync, "scalar": g.scalar}
+    seen = {}
+    left = {}
+    nprod = [0]
+
+    def need(q, sem, val):
+        if seen.get((q, sem), 0) < val:
+            queues[q].wait_ge(T.sem[sem], val)
+            seen[(q, sem)] = val
+
+    def partner(k):
+        return [c for c in groups[k] if topo.chip(c) == topo.chip(core)][0]
+
+    def engines(src, dsts):
+        m = topo.mask(src, dsts[0])
+        for d in dsts:
+            m &= topo.mask(src, d)
+        return m
+
+    def count(src, dsts):
+        return bin(engines(src, dsts)).count("1")
+
+    def send(op, dsts, out_ap, rsem, lsem):
+        ap, s, v = op
+        need("g", s, v)
+        m = engines(core, dsts)
+        if len(dsts) == 1:
+            rid, pid = topo.addr(dsts[0], core)
+            g.remote_dma(out_ap=out_ap, in_ap=ap, remote_sem=T.sem[rsem], local_sem=T.sem[lsem], pid=pid,
+                         routing_id=rid, dma_engine_mask=m)
+        else:
+            ids = [topo.addr(d, core) for d in dsts]
+            g.remote_dma_fused([RemoteDMATransfer(dst_ids=[DstId(rid=r, pnc=p) for r, p in ids], dma_engine_mask=m,
+                                                  remote_sem=T.sem[rsem], srcs=[ap], dsts=[out_ap for _ in dsts],
+                                                  alu_op=0)], local_sem=T.sem[lsem])
+        left[lsem] = left.get(lsem, 0) + bin(m).count("1")
+
+    def product(lhsT, rhs, n):
+        k = nprod[0]
+        nprod[0] += 1
+        need("tensor", lhsT[1], lhsT[2])
+        need("tensor", rhs[1], rhs[2])
+        g.tensor.matmul(T["ps%d" % k][:, 0:n], lhsT[0], rhs[0], True, True).then_inc(T.sem["t%d" % k], 1)
+        need("vector", "t%d" % k, 1)
+        g.vector.tensor_copy(T["sb%d" % k][:, 0:n], T["ps%d" % k][:, 0:n]).then_inc(T.sem["v%d" % k], 1)
+        return (T["sb%d" % k][:, 0:n], "v%d" % k, 1)
+
+    def store(op, after=None):
+        if after is not None:
+            need("sync", after, left[after])
+        need("sync", op[1], op[2])
+        g.sync.dma_start(T.y[:], op[0]).then_inc(T.sem.stored, 16)
+
+    def slot(k):
+        return T.gat[:, k * W:(k + 1) * W]
+
+    def takers(k, grp_i):
+        members = groups[grp_i]
+        return [c for i, c in enumerate(members) if i != k and (grp_i != last or i > k)]
+
+    def tile(k):
+        if k == j:
+            return (slot(k), "ld_a", 16)
+        return (slot(k), "a%d" % k, count(grp[k], takers(k, gi)))
+
+    feeder = {}
+    for t in range(2, len(groups)):
+        feeder[t] = [s for s in (1, 0) if topo.may_write(groups[s][0], groups[t][0])][0]
+
+    def landed_vector(src_group):
+        return (T.pl[:], "a_p", count(partner(src_group), [core]))
+
+    if gi == 0:
+        g.sync.dma_start(slot(j), T.m[:]).then_inc(T.sem.ld_a, 16)
+        if j == 0:
+            g.scalar.dma_start(T.xin[:], T.x[:]).then_inc(T.sem.ld_x, 16)
+            cur = product(tile(0), (T.xin[:], "ld_x", 16), F)
+            send(cur, takers(0, 0), T.pl[:], "a_p", "s1")
+        else:
+            send(tile(j), takers(j, 0), slot(j), "a%d" % j, "s1")
+            cur = (T.pl[:], "a_p", count(grp[0], takers(0, 0)))
+        mine = cur
+        for k in range(1, len(grp)):
+            cur = product(tile(k), cur, F)
+            if k == j:
+                mine = cur
+        send(cur, [partner(1)], T.pl[:], "a_p", "s2")
+        store(mine, after="s2")
+        p7 = product((T.gl[:], "a_g", count(partner(1), [core])), cur, F)
+        for t in feeder:
+            if feeder[t] == 0:
+                send(p7, [partner(t)], T.pl[:], "a_p", "s3")
+    else:
+        even = j % 2 == 0
+        g.sync.dma_start(slot(j), (T.mt if even else T.m)[:]).then_inc(T.sem.ld_a, 16)
+        if takers(j, gi):
+            send(tile(j), takers(j, gi), slot(j), "a%d" % j, "s1")
+        if even:
+            need("scalar", "s1", left["s1"])
+            g.scalar.dma_start(T.own2[:], T.m[:]).then_inc(T.sem.ld_b, 16)
+        own_m = (T.own2[:], "ld_b", 16)
+
+        whole = gi != last or j == 3
+        U = V = None
+        if whole:
+            if j < 2:
+                U = product(tile(1), tile(0), W)
+                V = product(tile(2), tile(3), W)
+            else:
+                V = product(tile(2), tile(3), W)
+                U = product(tile(1), tile(0), W)
+        elif j == 2:
+            U = product(tile(1), tile(0), W)
+
+        GT = None
+        if gi == 1:
+            GT = product(U, V, W)
+            send(GT, [partner(0)], T.gl[:], "a_g", "s2")
+        elif gi != last:
+            send(product(V, U, W), [partner(gi + 1)], T.gl[:], "a_g", "s2")
+
+        if j == 0:
+            LT = own_m
+        elif j == 1:
+            LT = product(tile(0), tile(1), W)
+        elif j == 2:
+            LT = product(U, own_m, W)
+        else:
+            LT = GT if GT is not None else product(U, V, W)
+
+        if gi == 1:
+            p3 = landed_vector(0)
+            p7 = product(GT, p3, F)
+            for t in feeder:
+                if feeder[t] == 1:
+                    send(p7, [partner(t)], T.pl[:], "a_p", "s3")
+            store(p7 if j == 3 else product(LT, p3, F), after="s3")
+        else:
+            if gi == last:
+                LT = product((T.gl[:], "a_g", count(partner(gi - 1), [core])), LT, W)
+            store(product(LT, landed_vector(feeder[gi]), F))
+
+    for s in left:
+        need("g", s, left[s])
+    need("sync", "stored", 16)

@@ -91,7 +91,12 @@ def rank_program(g, core, T, topo):
 
     def takers(k, grp_i):
         members = groups[grp_i]
-        return [c for i, c in enumerate(members) if i != k and (grp_i != last or i > k)]
+        places = [i for i in range(len(members)) if i != k and (grp_i != last or i > k)]
+        mate = [i for i in places if i // 2 == k // 2]
+        rest = [i for i in places if i // 2 != k // 2]
+        if k % 2:
+            rest.reverse()
+        return [members[i] for i in mate + rest]
 
     def tile(k):
         if k == j:
@@ -106,22 +111,26 @@ def rank_program(g, core, T, topo):
         return (T.pl[:], "a_p", count(partner(src_group), [core]))
 
     if gi == 0:
-        g.sync.dma_start(slot(j), T.m[:]).then_inc(T.sem.ld_a, 16)
+        g.sync.dma_start(slot(j), (T.mt if j == 2 else T.m)[:]).then_inc(T.sem.ld_a, 16)
         if j == 0:
             g.scalar.dma_start(T.xin[:], T.x[:]).then_inc(T.sem.ld_x, 16)
-            cur = product(tile(0), (T.xin[:], "ld_x", 16), F)
-            send(cur, takers(0, 0), T.pl[:], "a_p", "s1")
+            p0 = product(tile(0), (T.xin[:], "ld_x", 16), F)
+            send(p0, takers(0, 0), T.pl[:], "a_p", "s1")
         else:
             send(tile(j), takers(j, 0), slot(j), "a%d" % j, "s1")
-            cur = (T.pl[:], "a_p", count(grp[0], takers(0, 0)))
-        mine = cur
-        for k in range(1, len(grp)):
-            cur = product(tile(k), cur, F)
-            if k == j:
-                mine = cur
-        send(cur, [partner(1)], T.pl[:], "a_p", "s2")
+            p0 = (T.pl[:], "a_p", count(grp[0], takers(0, 0)))
+        if j == 2:
+            need("scalar", "s1", left["s1"])
+            g.scalar.dma_start(T.own2[:], T.m[:]).then_inc(T.sem.ld_b, 16)
+        Q = product(tile(2), tile(3), W)
+        p1 = product(tile(1), p0, F)
+        p3 = product(Q, p1, F)
+        send(p3, [partner(1)], T.pl[:], "a_p", "s2")
+        mine = [p0, p1, None, p3][j]
+        if mine is None:
+            mine = product((T.own2[:], "ld_b", 16), p1, F)
         store(mine, after="s2")
-        p7 = product((T.gl[:], "a_g", count(partner(1), [core])), cur, F)
+        p7 = product((T.gl[:], "a_g", count(partner(1), [core])), p3, F)
         for t in feeder:
             if feeder[t] == 0:
                 send(p7, [partner(t)], T.pl[:], "a_p", "s3")

from concourse.bass import DstId, RemoteDMATransfer

W = 128
NPROD = 6

SCRATCH = {
    "gat": ("sbuf", [128, 4 * W], "float32"),
    "own2": ("sbuf", [128, W], "float32"),
    "xin": ("sbuf", [128, 64], "float32"),
    "pl": ("sbuf", [128, 64], "float32"),
    "gl": ("sbuf", [128, W], "float32"),
}
for _k in range(NPROD):
    SCRATCH["ps%d" % _k] = ("psum", [128, 512], "float32")
    SCRATCH["sb%d" % _k] = ("sbuf", [128, W], "float32")

SEMAPHORES = (["ld_a", "ld_b", "ld_x", "a0", "a1", "a2", "a3", "a_p", "a_g", "s1", "s2", "s3", "stored"]
              + ["t%d" % _k for _k in range(NPROD)] + ["v%d" % _k for _k in range(NPROD)])


def rank_program(g, core, T, topo):
    if T.rank_of(core) is None:
        return
    cores = list(T.cores)
    hosts = []
    for c in cores:
        if topo.host(c) not in hosts:
            hosts.append(topo.host(c))
    groups = [[c for c in cores if topo.host(c) == h] for h in hosts]
    gi = hosts.index(topo.host(core))
    grp = groups[gi]
    j = grp.index(core)
    F = T.y.shape[1]
    last = len(groups) - 1

    queues = {"g": g, "tensor": g.tensor, "vector": g.vector, "sync": g.sync, "scalar": g.scalar}
    seen = {}
    left = {}
    nprod = [0]

    def need(q, sem, val):
        if seen.get((q, sem), 0) < val:
            queues[q].wait_ge(T.sem[sem], val)
            seen[(q, sem)] = val

    def partner(k):
        return [c for c in groups[k] if topo.chip(c) == topo.chip(core)][0]

    def engines(src, dsts):
        m = topo.mask(src, dsts[0])
        for d in dsts:
            m &= topo.mask(src, d)
        return m

    def count(src, dsts):
        return bin(engines(src, dsts)).count("1")

    def send(op, dsts, out_ap, rsem, lsem):
        ap, s, v = op
        need("g", s, v)
        m = engines(core, dsts)
        if len(dsts) == 1:
            rid, pid = topo.addr(dsts[0], core)
            g.remote_dma(out_ap=out_ap, in_ap=ap, remote_sem=T.sem[rsem], local_sem=T.sem[lsem], pid=pid,
                         routing_id=rid, dma_engine_mask=m)
        else:
            ids = [topo.addr(d, core) for d in dsts]
            g.remote_dma_fused([RemoteDMATransfer(dst_ids=[DstId(rid=r, pnc=p) for r, p in ids], dma_engine_mask=m,
                                                  remote_sem=T.sem[rsem], srcs=[ap], dsts=[out_ap for _ in dsts],
                                                  alu_op=0)], local_sem=T.sem[lsem])
        left[lsem] = left.get(lsem, 0) + bin(m).count("1")

    def product(lhsT, rhs, n):
        k = nprod[0]
        nprod[0] += 1
        need("tensor", lhsT[1], lhsT[2])
        need("tensor", rhs[1], rhs[2])
        g.tensor.matmul(T["ps%d" % k][:, 0:n], lhsT[0], rhs[0], True, True).then_inc(T.sem["t%d" % k], 1)
        need("vector", "t%d" % k, 1)
        g.vector.tensor_copy(T["sb%d" % k][:, 0:n], T["ps%d" % k][:, 0:n]).then_inc(T.sem["v%d" % k], 1)
        return (T["sb%d" % k][:, 0:n], "v%d" % k, 1)

    def store(op, after=None):
        if after is not None:
            need("sync", after, left[after])
        need("sync", op[1], op[2])
        g.sync.dma_start(T.y[:], op[0]).then_inc(T.sem.stored, 16)

    def slot(k):
        return T.gat[:, k * W:(k + 1) * W]

    def takers(k, grp_i):
        members = groups[grp_i]
        places = [i for i in range(len(members)) if i != k and (grp_i != last or i > k)]
        mate = [i for i in places if i // 2 == k // 2]
        rest = [i for i in places if i // 2 != k // 2]
        if k % 2:
            rest.reverse()
        return [members[i] for i in mate + rest]

    def tile(k):
        if k == j:
            return (slot(k), "ld_a", 16)
        return (slot(k), "a%d" % k, count(grp[k], takers(k, gi)))

    feeder = {}
    for t in range(2, len(groups)):
        feeder[t] = [s for s in (1, 0) if topo.may_write(groups[s][0], groups[t][0])][0]

    def landed_vector(src_group):
        return (T.pl[:], "a_p", count(partner(src_group), [core]))

    if gi == 0:
        g.sync.dma_start(slot(j), (T.mt if j == 2 else T.m)[:]).then_inc(T.sem.ld_a, 16)
        if j == 0:
            g.scalar.dma_start(T.xin[:], T.x[:]).then_inc(T.sem.ld_x, 16)
            p0 = product(tile(0), (T.xin[:], "ld_x", 16), F)
            send(p0, takers(0, 0), T.pl[:], "a_p", "s1")
        else:
            send(tile(j), takers(j, 0), slot(j), "a%d" % j, "s1")
            p0 = (T.pl[:], "a_p", count(grp[0], takers(0, 0)))
        if j == 2:
            need("scalar", "s1", left["s1"])
            g.scalar.dma_start(T.own2[:], T.m[:]).then_inc(T.sem.ld_b, 16)
        Q = product(tile(2), tile(3), W)
        p1 = product(tile(1), p0, F)
        p3 = product(Q, p1, F)
        send(p3, [partner(1)], T.pl[:], "a_p", "s2")
        mine = [p0, p1, None, p3][j]
        if mine is None:
            mine = product((T.own2[:], "ld_b", 16), p1, F)
        store(mine, after="s2")
        p7 = product((T.gl[:], "a_g", count(partner(1), [core])), p3, F)
        for t in feeder:
            if feeder[t] == 0:
                send(p7, [partner(t)], T.pl[:], "a_p", "s3")
    else:
        even = j % 2 == 0
        g.sync.dma_start(slot(j), (T.mt if even else T.m)[:]).then_inc(T.sem.ld_a, 16)
        if takers(j, gi):
            send(tile(j), takers(j, gi), slot(j), "a%d" % j, "s1")
        if even:
            need("scalar", "s1", left["s1"])
            g.scalar.dma_start(T.own2[:], T.m[:]).then_inc(T.sem.ld_b, 16)
        own_m = (T.own2[:], "ld_b", 16)

        whole = gi != last or j == 3
        U = V = None
        if whole:
            if j < 2:
                U = product(tile(1), tile(0), W)
                V = product(tile(2), tile(3), W)
            else:
                V = product(tile(2), tile(3), W)
                U = product(tile(1), tile(0), W)
        elif j == 2:
            U = product(tile(1), tile(0), W)

        GT = None
        if gi == 1:
            GT = product(U, V, W)
            send(GT, [partner(0)], T.gl[:], "a_g", "s2")
        elif gi != last:
            send(product(V, U, W), [partner(gi + 1)], T.gl[:], "a_g", "s2")

        if j == 0:
            LT = own_m
        elif j == 1:
            LT = product(tile(0), tile(1), W)
        elif j == 2:
            LT = product(U, own_m, W)
        else:
            LT = GT if GT is not None else product(U, V, W)

        if gi == 1:
            p3 = landed_vector(0)
            p7 = product(GT, p3, F)
            for t in feeder:
                if feeder[t] == 1:
                    send(p7, [partner(t)], T.pl[:], "a_p", "s3")
            store(p7 if j == 3 else product(LT, p3, F), after="s3")
        else:
            if gi == last:
                LT = product((T.gl[:], "a_g", count(partner(gi - 1), [core])), LT, W)
            store(product(LT, landed_vector(feeder[gi]), F))

    for s in left:
        need("g", s, left[s])
    need("sync", "stored", 16)
